import numpy as np
import ml_dtypes


def mxq(x, axis, fmt="e4m3"):
    dtype, down = {"e4m3": (ml_dtypes.float8_e4m3fn, 7), "e5m2": (ml_dtypes.float8_e5m2, 14)}[fmt]
    v = np.moveaxis(np.asarray(x, np.float32).astype(ml_dtypes.bfloat16).astype(np.float64), axis, -1)
    blocks = v.reshape(v.shape[:-1] + (-1, 32))
    amax = np.abs(blocks).max(-1, keepdims=True)
    byte = np.maximum(np.where(amax > 0, np.frexp(amax)[1] - 1 + 127, 0) - down, 1)
    scale = np.exp2(byte - 127.0)
    codes = (blocks / scale).astype(np.float32).astype(dtype).astype(np.float64)
    return np.moveaxis((codes * scale).reshape(v.shape), -1, axis)


WIDE = False


def mx_kscale(k):
    if not WIDE:
        return np.ones(k)
    levels = np.array([10, -10, 5, -5, 0])
    if k % 512:
        return np.exp2(np.random.permutation(np.resize(levels, k // 32))).repeat(32)
    a = np.empty((k // 512, 16))
    for p in range(k // 512):
        a[p, :8] = np.random.permutation(np.resize(levels, 8))
        for g in range(8):
            far = levels[np.abs(levels - a[p, g]) >= 10]
            a[p, g + 8] = far[np.random.randint(len(far))]
    return np.exp2(a.ravel()).repeat(32)


def f64(x):
    return np.asarray(x).astype(np.float64)


def striped(idx):
    return np.tile(idx.reshape(-1, 16).T, (8, 1)).astype(np.uint16)


def unstriped(offs):
    return offs[:16].T.reshape(-1).astype(np.int64)


def pack_weight(w):
    k, n = w.shape
    w = f64(np.asarray(w, np.float32).astype(ml_dtypes.bfloat16)).reshape(k // 32, 32, n)
    amax = np.abs(w).max(1)
    byte = np.clip(np.where(amax > 0, np.frexp(amax)[1] - 1 + 127 - 7, 1), 1, 254)
    scaled = (w * np.exp2(127.0 - byte)[:, None, :]).reshape(k, n).astype(np.float32)
    words = np.ascontiguousarray(scaled.reshape(k // 512, 128, 4, n).transpose(0, 1, 3, 2)).astype(ml_dtypes.float8_e4m3fn).view(np.uint8)
    return words, np.ascontiguousarray(byte.astype(np.uint8).reshape(k // 512, 16, n))


def unpack_weight(words, scales):
    g, p, n, _ = words.shape
    vals = np.ascontiguousarray(words).view(ml_dtypes.float8_e4m3fn).astype(np.float64) * np.repeat(np.exp2(scales.astype(np.float64) - 127.0), 8, axis=1)[..., None]
    return vals.transpose(0, 1, 3, 2).reshape(g * 512, n)


E2M1 = np.array([0.0, 0.5, 1.0, 1.5, 2.0, 3.0, 4.0, 6.0, -0.0, -0.5, -1.0, -1.5, -2.0, -3.0, -4.0, -6.0])


def pack_fp4(w):
    k, n = w.shape
    w = f64(np.asarray(w, np.float32).astype(ml_dtypes.bfloat16)).reshape(k // 32, 32, n)
    amax = np.abs(w).max(1)
    mant, ex = np.frexp(amax / 6.0)
    byte = np.clip(np.where(amax > 0, np.where(mant > 0.5, ex, ex - 1) + 127, 1), 1, 254)
    scaled = (w * np.exp2(127.0 - byte)[:, None, :]).reshape(k, n).astype(np.float32)
    c = np.ascontiguousarray(scaled.reshape(k // 512, 128, 4, n).transpose(0, 1, 3, 2)).astype(ml_dtypes.float4_e2m1fn).view(np.uint8) & 0xF
    words = (c[..., 0::2] | (c[..., 1::2] << 4)).reshape(k // 512, 128, 2 * n)
    return np.ascontiguousarray(words), np.ascontiguousarray(byte.astype(np.uint8).reshape(k // 512, 16, n))


def unpack_fp4(words, scales):
    g, _, n = scales.shape
    words = np.ascontiguousarray(words).reshape(g, 128, n, 2)
    nib = np.empty((g, 128, n, 4), np.uint8)
    nib[..., 0::2] = words & 0xF
    nib[..., 1::2] = words >> 4
    vals = E2M1[nib] * np.repeat(np.exp2(scales.astype(np.float64) - 127.0), 8, axis=1)[..., None]
    return vals.transpose(0, 1, 3, 2).reshape(g * 512, n)


def relu(v):
    return np.maximum(v, 0.0)


K, T, S, D, N, H = 512, 2048, 512, 4, 256, 512


def setup_inputs():
    n = np.random.standard_normal
    s = mx_kscale(K)[:, None]
    u = mx_kscale(H)
    packed_xT = pack_weight(n((K, T)) * s)
    packed_w1 = pack_fp4(n((K, H)) / np.sqrt(K) / s)
    packed_w2 = pack_fp4(n((H, N)) / np.sqrt(H) / u[:, None])
    return {
        "x_words": packed_xT[0],
        "x_scales": packed_xT[1],
        "w1_words": packed_w1[0],
        "w1_scales": packed_w1[1],
        "noise": (np.random.uniform(0.3, 1.0, (H, S))).astype(np.float32),
        "unit": (np.random.uniform(0.6, 1.4, (H, 1)) * u[:, None]).astype(np.float32),
        "w2_words": packed_w2[0],
        "w2_scales": packed_w2[1],
        "offs": striped(np.random.permutation(T)[:S]),
        "itf": striped(np.random.permutation(S)),
    }


def reference(x_words, x_scales, w1_words, w1_scales, noise, unit, w2_words, w2_scales, offs, itf):
    xq = unpack_weight(x_words, x_scales)[:, unstriped(offs)]
    y = unpack_fp4(w1_words, w1_scales).T @ xq
    gain = np.log(np.exp(y) + 1.0) + 0.2
    inv = f64(noise) / gain
    lvl = 0.25 * (inv.reshape(len(inv), -1, D).sum(axis=2) + 2.0)
    pw1 = relu(np.repeat(lvl, D, axis=1) - inv)
    exc = -1.0 * (pw1.reshape(len(pw1), -1, D).sum(axis=2)) + 2.0
    pw2 = relu(pw1 + 0.25 * np.repeat(exc, D, axis=1))
    rate = np.log(pw2 / inv + 1.0)
    hid = f64(unit) * ((rate / (np.repeat(rate.reshape(len(rate), -1, D).sum(axis=2), D, axis=1) + 0.5)) * gain[:, unstriped(itf)])
    return unpack_fp4(w2_words, w2_scales).T @ mxq(hid, 0, "e4m3")

@@ -1,0 +1,293 @@
+import math
+from contextlib import ExitStack
+
+import concourse.mybir as mybir
+
+K, T, S, D, N, H = 512, 2048, 512, 4, 256, 512
+FLOPS = 2 * K * H * S + 2 * H * N * S
+
+F32 = mybir.dt.float32
+BF16 = mybir.dt.bfloat16
+I32 = mybir.dt.int32
+U32 = mybir.dt.uint32
+U16 = mybir.dt.uint16
+U8 = mybir.dt.uint8
+FP8X4 = mybir.dt.float8_e4m3fn_x4
+FP4X4 = mybir.dt.float4_e2m1fn_x4
+ACT = mybir.ActivationFunctionType
+ALU = mybir.AluOpType
+
+P = 128
+PACK = 4
+HALF = S // 2
+LIST = 16
+W = 128
+NQ = S // W
+Q = PACK * W
+EXP_CAP = 2.0 ** 60
+GAIN_FLOOR = 0.2
+ON_VECTOR = 3
+
+
+def tile_picked_ywater_shr_p_kernel(
+    tc, x_words, x_scales, w1_words, w1_scales, noise, unit, w2_words, w2_scales, offs, itf, out
+):
+    nc = tc.nc
+    with ExitStack() as ctx:
+        keep = ctx.enter_context(tc.tile_pool(name="keep", bufs=1))
+        psum = ctx.enter_context(tc.psum_pool(name="psum", bufs=1))
+
+        def sb(shape, dtype, name):
+            return keep.tile(shape, dtype, name=name, align_bytes=64)
+
+        def load_scale_rows(queues, plane, rows):
+            for q, queue in enumerate(queues):
+                queue.dma_start(
+                    out=plane[32 * q : 32 * q + 4, :].bitcast(I32), in_=rows[0, 4 * q : 4 * q + 4, :].bitcast(I32)
+                )
+
+        def shared(shape, dtype, name, tag):
+            return keep.tile(shape, dtype, name=name, tag=tag, align_bytes=64)
+
+        offs_sb = sb([P, S // LIST], U16, "offs_sb")
+        itf_sb = sb([P, S // LIST], U16, "itf_sb")
+        xw = sb([P, T], I32, "xw")
+        xs = sb([P, T], U8, "xs")
+        w1w_raw = sb([P, 2 * H], U8, "w1w_raw")
+        w1s_raw = shared([P, H], U8, "w1s_raw", "early")
+        unit_sb = sb([P, PACK], F32, "unit_sb")
+
+        nc.vector.memset(xs[:, : T // 2].bitcast(I32), 0)
+        nc.gpsimd.memset(xs[:, T // 2 :].bitcast(I32), 0)
+        nc.gpsimd.memset(w1s_raw[:].bitcast(I32), 0)
+
+        nc.sync.dma_start(offs_sb[:], offs)
+        nc.sync.dma_start(out=w1w_raw[:].bitcast(I32), in_=w1_words[0].bitcast(I32))
+        nc.sync.dma_start(out=unit_sb[:], in_=unit.rearrange("(p t) o -> p (t o)", t=PACK))
+        load_scale_rows([nc.sync] * 4, xs, x_scales)
+        nc.sync.dma_start(out=xw[:], in_=x_words[0].rearrange("p n t -> p (n t)").bitcast(I32))
+        load_scale_rows([nc.sync] * 4, w1s_raw, w1_scales)
+        nc.sync.dma_start(itf_sb[:], itf)
+
+        w1w = sb([P, 2 * H], U8, "w1w")
+        w1s = sb([P, H], U8, "w1s")
+        nc.vector.tensor_copy(
+            out=w1w[:].rearrange("p (t m b) -> p t m b", t=PACK, b=2),
+            in_=w1w_raw[:].rearrange("p (m t b) -> p t m b", t=PACK, b=2),
+        )
+        nc.gpsimd.tensor_copy(
+            out=w1s[:].rearrange("p (t m) -> p t m", t=PACK), in_=w1s_raw[:].rearrange("p (m t) -> p t m", t=PACK)
+        )
+
+        noise_sb = shared([P, PACK * S], F32, "noise_sb", "early")
+        nc.sync.dma_start(out=noise_sb[:], in_=noise.rearrange("(p t) j -> p (t j)", t=PACK))
+
+        unit_rows = sb([P, ON_VECTOR, HALF], F32, "unit_rows")
+        nc.scalar.activation(
+            out=unit_rows[:], in_=unit_sb[:, :ON_VECTOR].unsqueeze(2).broadcast_to([P, ON_VECTOR, HALF]), func=ACT.Copy
+        )
+
+        cols = HALF // LIST
+        e = shared([P, PACK * S], F32, "e", "exp")
+        xg_s = [sb([P, HALF], U8, "xg_s%d" % h) for h in range(2)]
+        xg_w = [sb([P, HALF], U32, "xg_w%d" % h) for h in range(2)]
+        for h in range(2):
+            nc.vector.tensor_copy(xg_s[h][:], xs[:].indirect(offs_sb[:, h * cols : (h + 1) * cols]))
+        for h in range(2):
+            nc.vector.tensor_copy(xg_w[h][:], xw[:].bitcast(U32).indirect(offs_sb[:, h * cols : (h + 1) * cols]))
+        y = [psum.tile([P, S], F32, name="y%d" % t) for t in range(PACK)]
+        for t, h in [(0, 0), (1, 0), (0, 1), (1, 1), (2, 0), (2, 1), (3, 0), (3, 1)]:
+            nc.tensor.matmul_mx(
+                out=y[t][:, h * HALF : (h + 1) * HALF],
+                lhsT=w1w[:, 2 * P * t : 2 * P * (t + 1)].bitcast(FP4X4),
+                lhsT_scale=w1s[:, P * t : P * (t + 1)],
+                rhs=xg_w[h][:].bitcast(FP8X4),
+                rhs_scale=xg_s[h][:],
+                start=True,
+                stop=True,
+            )
+        for t in range(PACK):
+            nc.scalar.activation(out=e[:, t * S : (t + 1) * S], in_=y[t][:], func=ACT.Exp)
+        ec = shared([P, PACK * S], F32, "ec", "capped")
+        for t in range(PACK):
+            nc.vector.tensor_scalar(
+                out=ec[:, t * S : (t + 1) * S], in0=e[:, t * S : (t + 1) * S], scalar1=EXP_CAP, scalar2=None, op0=ALU.min
+            )
+
+        soft = sb([P, PACK * S], F32, "soft")
+        log_gain = sb([P, PACK * S], F32, "log_gain")
+        gain = [sb([P, S], F32, "gain%d" % t) for t in range(PACK)]
+        c = math.exp(GAIN_FLOOR)
+        for t in range(PACK):
+            nc.scalar.activation(
+                out=soft[:, t * S : (t + 1) * S], in_=ec[:, t * S : (t + 1) * S], func=ACT.Ln, scale=c, bias=c
+            )
+        for t in range(PACK):
+            nc.vector.scalar_tensor_tensor(
+                out=gain[t][:], in0=y[t][:], scalar=GAIN_FLOOR, in1=soft[:, t * S : (t + 1) * S],
+                op0=ALU.add, op1=ALU.max,
+            )
+            nc.scalar.activation(out=log_gain[:, t * S : (t + 1) * S], in_=gain[t][:], func=ACT.Ln)
+
+        w2w = shared([P, 2 * N], U8, "w2w", "exp")
+        w2s = shared([P, N], U8, "w2s", "capped")
+        nc.gpsimd.memset(w2s[:].bitcast(I32), 0)
+        nc.sync.dma_start(out=w2w[:].bitcast(I32), in_=w2_words[0].bitcast(I32))
+        load_scale_rows([nc.sync] * 4, w2s, w2_scales)
+
+        fetched = sb([P, PACK * S], F32, "fetched")
+        for h in range(2):
+            for t in range(ON_VECTOR):
+                nc.vector.tensor_tensor(
+                    fetched[:, t * S + h * HALF : t * S + (h + 1) * HALF],
+                    gain[t][:].indirect(itf_sb[:, h * cols : (h + 1) * cols]),
+                    unit_rows[:, t, :],
+                    ALU.mult,
+                )
+
+        def planes(tile, h):
+            return tile[:].rearrange("p (t j) -> p t j", t=PACK)[:, :, h * HALF : (h + 1) * HALF]
+
+        def part(tile, h, width):
+            return tile[:, h * width : (h + 1) * width]
+
+        BIG = PACK * HALF
+        SMALL = BIG // D
+        rgain = sb([P, PACK * S], F32, "rgain")
+        inv = sb([P, PACK * S], F32, "inv")
+        low = sb([P, PACK * S], F32, "low")
+        pairs1 = sb([P, PACK * S // 2], F32, "pairs1")
+        pairs2 = sb([P, PACK * S // 2], F32, "pairs2")
+        sum1 = sb([P, S], F32, "sum1")
+        sum2 = sb([P, S], F32, "sum2")
+        log_inv = sb([P, PACK * S], F32, "log_inv")
+        log_lvl = sb([P, S], F32, "log_lvl")
+        fetched4 = sb([P, PACK * S], F32, "fetched4")
+        for h in range(2):
+            nc.scalar.activation(
+                out=part(rgain, h, BIG).rearrange("p (t j) -> p t j", t=PACK), in_=planes(log_gain, h),
+                func=ACT.Exp, scale=-1.0,
+            )
+
+        def add_pairs(pairs, src, h):
+            four = part(src, h, BIG).rearrange("p (g d) -> p g d", d=D)
+            two = part(pairs, h, BIG // 2).rearrange("p (g d) -> p g d", d=2)
+            nc.vector.tensor_tensor(out=two, in0=four[:, :, 0:2], in1=four[:, :, 2:4], op=ALU.add)
+
+        def add_two(dst, pairs, h):
+            two = part(pairs, h, BIG // 2).rearrange("p (g d) -> p g d", d=2)
+            nc.vector.scalar_tensor_tensor(
+                out=part(dst, h, SMALL), in0=two[:, :, 0], scalar=2.0, in1=two[:, :, 1], op0=ALU.add, op1=ALU.add
+            )
+
+        for h in range(2):
+            nc.vector.tensor_tensor(
+                out=part(inv, h, BIG).rearrange("p (t j) -> p t j", t=PACK),
+                in0=part(rgain, h, BIG).rearrange("p (t j) -> p t j", t=PACK),
+                in1=planes(noise_sb, h), op=ALU.mult,
+            )
+        for h in range(2):
+            add_pairs(pairs1, inv, h)
+        for h in range(2):
+            add_two(sum1, pairs1, h)
+        for h in range(2):
+            nc.vector.scalar_tensor_tensor(
+                out=part(low, h, BIG).rearrange("p (g d) -> p g d", d=D),
+                in0=part(sum1, h, SMALL).unsqueeze(2).broadcast_to([P, SMALL, D]),
+                scalar=0.25,
+                in1=part(inv, h, BIG).rearrange("p (g d) -> p g d", d=D),
+                op0=ALU.mult, op1=ALU.min,
+            )
+        for h in range(2):
+            add_pairs(pairs2, low, h)
+        for h in range(2):
+            add_two(sum2, pairs2, h)
+        for h in range(2):
+            nc.scalar.activation(
+                out=part(log_inv, h, BIG).rearrange("p (j t) -> p j t", t=PACK),
+                in_=part(inv, h, BIG).rearrange("p (t j) -> p j t", t=PACK), func=ACT.Ln,
+            )
+        for h in range(2):
+            nc.scalar.activation(
+                out=part(log_lvl, h, SMALL).rearrange("p (v t) -> p v t", t=PACK),
+                in_=part(sum2, h, SMALL).rearrange("p (t v) -> p v t", t=PACK), func=ACT.Ln, scale=0.25,
+            )
+        for t in range(ON_VECTOR, PACK):
+            scaled = sb([P, S], F32, "scaled%d" % t)
+            nc.scalar.activation(out=scaled[:], in_=gain[t][:], func=ACT.Copy, scale=unit_sb[:, t : t + 1])
+            for h in range(2):
+                nc.scalar.activation(
+                    fetched[:, t * S + h * HALF : t * S + (h + 1) * HALF],
+                    scaled[:].indirect(itf_sb[:, h * cols : (h + 1) * cols]),
+                    ACT.Copy,
+                )
+        for q in range(NQ):
+            nc.scalar.activation(
+                out=part(fetched4, q, Q).rearrange("p (j t) -> p j t", t=PACK),
+                in_=fetched[:].rearrange("p (t j) -> p j t", t=PACK)[:, q * W : (q + 1) * W, :], func=ACT.Copy,
+            )
+
+        raw = sb([P, PACK * S], F32, "raw")
+        acc = [sb([P, S], F32, "acc%d" % d) for d in range(D)]
+        log_den = sb([P, S], F32, "log_den")
+        rden = sb([P, S], F32, "rden")
+        num = sb([P, PACK * S], F32, "num")
+
+        def vdt(tile, q, width):
+            return part(tile, q, width).rearrange("p (v d t) -> p v d t", d=D, t=PACK)
+
+        def vt(tile, q, width):
+            return part(tile, q, width).rearrange("p (v t) -> p v t", t=PACK)
+
+        def over_d(tile, q, width):
+            return vt(tile, q, width).unsqueeze(2).broadcast_to([P, width // PACK, D, PACK])
+
+        for h in range(2):
+            nc.vector.tensor_tensor(
+                out=vdt(raw, h, BIG), in0=over_d(log_lvl, h, SMALL), in1=vdt(log_inv, h, BIG), op=ALU.subtract
+            )
+        for d in range(D):
+            for h in range(2):
+                src = vdt(raw, h, BIG)[:, :, d, :]
+                if d == 0:
+                    nc.vector.tensor_scalar(
+                        out=vt(acc[d], h, SMALL), in0=src, scalar1=0.0, scalar2=0.5, op0=ALU.max, op1=ALU.add
+                    )
+                else:
+                    nc.vector.scalar_tensor_tensor(
+                        out=vt(acc[d], h, SMALL), in0=src, scalar=0.0, in1=vt(acc[d - 1], h, SMALL),
+                        op0=ALU.max, op1=ALU.add,
+                    )
+        for h in range(2):
+            nc.scalar.activation(out=part(log_den, h, SMALL), in_=part(acc[D - 1], h, SMALL), func=ACT.Ln)
+        nc.scalar.activation(out=rden[:], in_=log_den[:], func=ACT.Exp, scale=-1.0)
+        for h in range(2):
+            nc.vector.scalar_tensor_tensor(
+                out=part(num, h, BIG), in0=part(raw, h, BIG), scalar=0.0, in1=part(fetched4, h, BIG),
+                op0=ALU.max, op1=ALU.mult,
+            )
+
+        out3 = out.rearrange("(m p) j -> p m j", p=P)
+        for q in range(NQ):
+            hid = sb([P, Q], BF16, "hid%d" % q)
+            codes = sb([P, W], U32, "codes%d" % q)
+            scales = sb([P, W], U8, "scales%d" % q)
+            nc.vector.tensor_tensor(
+                out=hid[:].rearrange("p (v d t) -> p v d t", d=D, t=PACK), in0=vdt(num, q, Q), in1=over_d(rden, q, W),
+                op=ALU.mult,
+            )
+            nc.vector.quantize_mx(out=codes[:].bitcast(FP8X4), scales=scales[:], in_=hid[:])
+            bank = psum.tile([P, N // P, W], F32, name="o%d" % q)
+            for m in range(N // P):
+                nc.tensor.matmul_mx(
+                    out=bank[:, m, :],
+                    lhsT=w2w[:, 2 * P * m : 2 * P * (m + 1)].bitcast(FP4X4),
+                    lhsT_scale=w2s[:, P * m : P * (m + 1)],
+                    rhs=codes[:].bitcast(FP8X4),
+                    rhs_scale=scales[:],
+                    start=True,
+                    stop=True,
+                )
+            res = sb([P, N // P, W], F32, "res%d" % q)
+            nc.scalar.copy(out=res[:], in_=bank[:])
+            nc.sync.dma_start(out=out3[:, :, q * W : (q + 1) * W], in_=res[:])

@@ -2,6 +2,7 @@ import math
 from contextlib import ExitStack
 
 import concourse.mybir as mybir
+from concourse.masks import make_identity
 
 K, T, S, D, N, H = 512, 2048, 512, 4, 256, 512
 FLOPS = 2 * K * H * S + 2 * H * N * S
@@ -26,7 +27,6 @@ NQ = S // W
 Q = PACK * W
 EXP_CAP = 2.0 ** 60
 GAIN_FLOOR = 0.2
-ON_VECTOR = 3
 
 
 def tile_picked_ywater_shr_p_kernel(
@@ -63,11 +63,11 @@ def tile_picked_ywater_shr_p_kernel(
 
         nc.sync.dma_start(offs_sb[:], offs)
         nc.sync.dma_start(out=w1w_raw[:].bitcast(I32), in_=w1_words[0].bitcast(I32))
-        nc.sync.dma_start(out=unit_sb[:], in_=unit.rearrange("(p t) o -> p (t o)", t=PACK))
         load_scale_rows([nc.sync] * 4, xs, x_scales)
         nc.sync.dma_start(out=xw[:], in_=x_words[0].rearrange("p n t -> p (n t)").bitcast(I32))
         load_scale_rows([nc.sync] * 4, w1s_raw, w1_scales)
         nc.sync.dma_start(itf_sb[:], itf)
+        nc.sync.dma_start(out=unit_sb[:], in_=unit.rearrange("(p t) o -> p (t o)", t=PACK))
 
         w1w = sb([P, 2 * H], U8, "w1w")
         w1s = sb([P, H], U8, "w1s")
@@ -82,10 +82,11 @@ def tile_picked_ywater_shr_p_kernel(
         noise_sb = shared([P, PACK * S], F32, "noise_sb", "early")
         nc.sync.dma_start(out=noise_sb[:], in_=noise.rearrange("(p t) j -> p (t j)", t=PACK))
 
-        unit_rows = sb([P, ON_VECTOR, HALF], F32, "unit_rows")
-        nc.scalar.activation(
-            out=unit_rows[:], in_=unit_sb[:, :ON_VECTOR].unsqueeze(2).broadcast_to([P, ON_VECTOR, HALF]), func=ACT.Copy
-        )
+        def bank(shape, name):
+            return psum.tile(shape, F32, name=name, tag="bank", bufs=8)
+
+        ident = sb([P, P], F32, "ident")
+        make_identity(nc, ident[:])
 
         cols = HALF // LIST
         e = shared([P, PACK * S], F32, "e", "exp")
@@ -95,7 +96,7 @@ def tile_picked_ywater_shr_p_kernel(
             nc.vector.tensor_copy(xg_s[h][:], xs[:].indirect(offs_sb[:, h * cols : (h + 1) * cols]))
         for h in range(2):
             nc.vector.tensor_copy(xg_w[h][:], xw[:].bitcast(U32).indirect(offs_sb[:, h * cols : (h + 1) * cols]))
-        y = [psum.tile([P, S], F32, name="y%d" % t) for t in range(PACK)]
+        y = [bank([P, S], "y%d" % t) for t in range(PACK)]
         for t, h in [(0, 0), (1, 0), (0, 1), (1, 1), (2, 0), (2, 1), (3, 0), (3, 1)]:
             nc.tensor.matmul_mx(
                 out=y[t][:, h * HALF : (h + 1) * HALF],
@@ -115,8 +116,7 @@ def tile_picked_ywater_shr_p_kernel(
             )
 
         soft = sb([P, PACK * S], F32, "soft")
-        log_gain = sb([P, PACK * S], F32, "log_gain")
-        gain = [sb([P, S], F32, "gain%d" % t) for t in range(PACK)]
+        gain = sb([P, PACK * S], F32, "gain")
         c = math.exp(GAIN_FLOOR)
         for t in range(PACK):
             nc.scalar.activation(
@@ -124,10 +124,9 @@ def tile_picked_ywater_shr_p_kernel(
             )
         for t in range(PACK):
             nc.vector.scalar_tensor_tensor(
-                out=gain[t][:], in0=y[t][:], scalar=GAIN_FLOOR, in1=soft[:, t * S : (t + 1) * S],
+                out=gain[:, t * S : (t + 1) * S], in0=y[t][:], scalar=GAIN_FLOOR, in1=soft[:, t * S : (t + 1) * S],
                 op0=ALU.add, op1=ALU.max,
             )
-            nc.scalar.activation(out=log_gain[:, t * S : (t + 1) * S], in_=gain[t][:], func=ACT.Ln)
 
         w2w = shared([P, 2 * N], U8, "w2w", "exp")
         w2s = shared([P, N], U8, "w2s", "capped")
@@ -135,103 +134,8 @@ def tile_picked_ywater_shr_p_kernel(
         nc.sync.dma_start(out=w2w[:].bitcast(I32), in_=w2_words[0].bitcast(I32))
         load_scale_rows([nc.sync] * 4, w2s, w2_scales)
 
-        fetched = sb([P, PACK * S], F32, "fetched")
-        for h in range(2):
-            for t in range(ON_VECTOR):
-                nc.vector.tensor_tensor(
-                    fetched[:, t * S + h * HALF : t * S + (h + 1) * HALF],
-                    gain[t][:].indirect(itf_sb[:, h * cols : (h + 1) * cols]),
-                    unit_rows[:, t, :],
-                    ALU.mult,
-                )
-
-        def planes(tile, h):
-            return tile[:].rearrange("p (t j) -> p t j", t=PACK)[:, :, h * HALF : (h + 1) * HALF]
-
         def part(tile, h, width):
             return tile[:, h * width : (h + 1) * width]
-
-        BIG = PACK * HALF
-        SMALL = BIG // D
-        rgain = sb([P, PACK * S], F32, "rgain")
-        inv = sb([P, PACK * S], F32, "inv")
-        low = sb([P, PACK * S], F32, "low")
-        pairs1 = sb([P, PACK * S // 2], F32, "pairs1")
-        pairs2 = sb([P, PACK * S // 2], F32, "pairs2")
-        sum1 = sb([P, S], F32, "sum1")
-        sum2 = sb([P, S], F32, "sum2")
-        log_inv = sb([P, PACK * S], F32, "log_inv")
-        log_lvl = sb([P, S], F32, "log_lvl")
-        fetched4 = sb([P, PACK * S], F32, "fetched4")
-        for h in range(2):
-            nc.scalar.activation(
-                out=part(rgain, h, BIG).rearrange("p (t j) -> p t j", t=PACK), in_=planes(log_gain, h),
-                func=ACT.Exp, scale=-1.0,
-            )
-
-        def add_pairs(pairs, src, h):
-            four = part(src, h, BIG).rearrange("p (g d) -> p g d", d=D)
-            two = part(pairs, h, BIG // 2).rearrange("p (g d) -> p g d", d=2)
-            nc.vector.tensor_tensor(out=two, in0=four[:, :, 0:2], in1=four[:, :, 2:4], op=ALU.add)
-
-        def add_two(dst, pairs, h):
-            two = part(pairs, h, BIG // 2).rearrange("p (g d) -> p g d", d=2)
-            nc.vector.scalar_tensor_tensor(
-                out=part(dst, h, SMALL), in0=two[:, :, 0], scalar=2.0, in1=two[:, :, 1], op0=ALU.add, op1=ALU.add
-            )
-
-        for h in range(2):
-            nc.vector.tensor_tensor(
-                out=part(inv, h, BIG).rearrange("p (t j) -> p t j", t=PACK),
-                in0=part(rgain, h, BIG).rearrange("p (t j) -> p t j", t=PACK),
-                in1=planes(noise_sb, h), op=ALU.mult,
-            )
-        for h in range(2):
-            add_pairs(pairs1, inv, h)
-        for h in range(2):
-            add_two(sum1, pairs1, h)
-        for h in range(2):
-            nc.vector.scalar_tensor_tensor(
-                out=part(low, h, BIG).rearrange("p (g d) -> p g d", d=D),
-                in0=part(sum1, h, SMALL).unsqueeze(2).broadcast_to([P, SMALL, D]),
-                scalar=0.25,
-                in1=part(inv, h, BIG).rearrange("p (g d) -> p g d", d=D),
-                op0=ALU.mult, op1=ALU.min,
-            )
-        for h in range(2):
-            add_pairs(pairs2, low, h)
-        for h in range(2):
-            add_two(sum2, pairs2, h)
-        for h in range(2):
-            nc.scalar.activation(
-                out=part(log_inv, h, BIG).rearrange("p (j t) -> p j t", t=PACK),
-                in_=part(inv, h, BIG).rearrange("p (t j) -> p j t", t=PACK), func=ACT.Ln,
-            )
-        for h in range(2):
-            nc.scalar.activation(
-                out=part(log_lvl, h, SMALL).rearrange("p (v t) -> p v t", t=PACK),
-                in_=part(sum2, h, SMALL).rearrange("p (t v) -> p v t", t=PACK), func=ACT.Ln, scale=0.25,
-            )
-        for t in range(ON_VECTOR, PACK):
-            scaled = sb([P, S], F32, "scaled%d" % t)
-            nc.scalar.activation(out=scaled[:], in_=gain[t][:], func=ACT.Copy, scale=unit_sb[:, t : t + 1])
-            for h in range(2):
-                nc.scalar.activation(
-                    fetched[:, t * S + h * HALF : t * S + (h + 1) * HALF],
-                    scaled[:].indirect(itf_sb[:, h * cols : (h + 1) * cols]),
-                    ACT.Copy,
-                )
-        for q in range(NQ):
-            nc.scalar.activation(
-                out=part(fetched4, q, Q).rearrange("p (j t) -> p j t", t=PACK),
-                in_=fetched[:].rearrange("p (t j) -> p j t", t=PACK)[:, q * W : (q + 1) * W, :], func=ACT.Copy,
-            )
-
-        raw = sb([P, PACK * S], F32, "raw")
-        acc = [sb([P, S], F32, "acc%d" % d) for d in range(D)]
-        log_den = sb([P, S], F32, "log_den")
-        rden = sb([P, S], F32, "rden")
-        num = sb([P, PACK * S], F32, "num")
 
         def vdt(tile, q, width):
             return part(tile, q, width).rearrange("p (v d t) -> p v d t", d=D, t=PACK)
@@ -242,10 +146,123 @@ def tile_picked_ywater_shr_p_kernel(
         def over_d(tile, q, width):
             return vt(tile, q, width).unsqueeze(2).broadcast_to([P, width // PACK, D, PACK])
 
-        for h in range(2):
+        def pairs_of(tile, q):
+            return tile[:].rearrange("p (t q u e) -> p q t u e", t=PACK, q=NQ, e=2)[:, q]
+
+        BIG = PACK * HALF
+        SMALL = BIG // D
+        V = W // D
+        pair = sb([P, PACK * S // 2], F32, "pair")
+        power = sb([P, S], F32, "power")
+        cross = sb([P, PACK * S], F32, "cross")
+        inv = sb([P, PACK * S], F32, "inv")
+        low = sb([P, PACK * S], F32, "low")
+        log_inv = sb([P, PACK * S], F32, "log_inv")
+        raw = sb([P, PACK * S], F32, "raw")
+        fetched = [sb([P, PACK * HALF], F32, "fetched%d" % h) for h in range(2)]
+        fetched4 = sb([P, PACK * S], F32, "fetched4")
+        acc = [sb([P, S], F32, "acc%d" % d) for d in range(D)]
+        log_den = sb([P, S], F32, "log_den")
+        rden = sb([P, S], F32, "rden")
+        rden1 = sb([P, S], F32, "rden1")
+        num = sb([P, PACK * S], F32, "num")
+
+        def dg(tile, q):
+            return part(tile, q, Q).rearrange("p (d g) -> p d g", d=D)
+
+        def scaled_inverse(q):
+            g = pairs_of(gain, q)
             nc.vector.tensor_tensor(
-                out=vdt(raw, h, BIG), in0=over_d(log_lvl, h, SMALL), in1=vdt(log_inv, h, BIG), op=ALU.subtract
+                out=part(pair, q, Q // 2).rearrange("p (t u) -> p t u", t=PACK), in0=g[:, :, :, 0], in1=g[:, :, :, 1],
+                op=ALU.mult,
             )
+            nc.vector.tensor_tensor(
+                out=part(cross, q, Q).rearrange("p (e t u) -> p e t u", t=PACK, e=2),
+                in0=pairs_of(noise_sb, q).rearrange("p t u e -> p e t u"),
+                in1=g.rearrange("p t u e -> p e t u")[:, ::-1], op=ALU.mult,
+            )
+            halves = part(pair, q, Q // 2).rearrange("p (g h) -> p h g", h=2)
+            nc.vector.scalar_tensor_tensor(
+                out=part(power, q, W), in0=halves[:, 0, :], scalar=2.0, in1=halves[:, 1, :], op0=ALU.mult, op1=ALU.mult
+            )
+            nc.vector.tensor_tensor(
+                out=part(inv, q, Q).rearrange("p (h e g) -> p h e g", h=2, e=2),
+                in0=part(cross, q, Q).rearrange("p (e g h) -> p h e g", h=2, e=2),
+                in1=halves[:, ::-1, :].unsqueeze(2).broadcast_to([P, 2, 2, W]),
+                op=ALU.mult,
+            )
+
+        def add_turned(members, name):
+            total = bank([P, W], name)
+            for n, member in enumerate(members):
+                nc.tensor.matmul(
+                    total[:], lhsT=member, rhs=ident[:], is_transpose=True, start=(n == 0), stop=(n == len(members) - 1)
+                )
+            return total
+
+        def first_level(q, minus8):
+            total = add_turned([part(power, q, W)] + [dg(inv, q)[:, d, :] for d in range(D)], "first%d" % q)
+            nc.scalar.activation(out=minus8, in_=total[:], func=ACT.Copy, scale=-2.0)
+            turned = bank([P, D, W], "turned%d" % q)
+            for d in range(D):
+                nc.tensor.transpose(turned[:, d, :], dg(inv, q)[:, d, :], ident[:])
+            return turned
+
+        def second_level(q, minus8, turned):
+            nc.vector.scalar_tensor_tensor(
+                out=dg(low, q), in0=minus8.unsqueeze(1).broadcast_to([P, D, W]), scalar=-0.125, in1=turned[:],
+                op0=ALU.mult, op1=ALU.max,
+            )
+            total = add_turned([minus8] + [dg(low, q)[:, d, :] for d in range(D)], "second%d" % q)
+            nc.scalar.activation(
+                out=vt(log_lvl[q], 0, W), in_=total[:].rearrange("p (t v) -> p v t", t=PACK), func=ACT.Ln, scale=-0.25
+            )
+
+        def log_of_inverse(q):
+            nc.scalar.activation(
+                out=part(log_inv, q, Q).rearrange("p (v d t) -> p d v t", d=D, t=PACK),
+                in_=part(inv, q, Q).rearrange("p (d t v) -> p d v t", d=D, t=PACK),
+                func=ACT.Ln,
+            )
+
+        def raw_rate(q):
+            nc.vector.tensor_tensor(
+                out=vdt(raw, q, Q), in0=over_d(log_lvl[q], 0, W), in1=vdt(log_inv, q, Q), op=ALU.subtract
+            )
+
+        spare = sb([P, 2 * W], F32, "spare")
+        log_lvl = [
+            fetched4[:, Q - W // 2 : Q + W // 2], fetched4[:, 3 * Q - W // 2 : 3 * Q + W // 2], spare[:, :W], spare[:, W:]
+        ]
+        minus8 = [fetched[1][:, q * HALF : q * HALF + W] for q in range(NQ)]
+        turned = {}
+        LAG = 2
+        for step in range(NQ + 2 * LAG):
+            if step < NQ:
+                scaled_inverse(step)
+                turned[step] = first_level(step, minus8[step])
+                log_of_inverse(step)
+            q = step - LAG
+            if 0 <= q < NQ:
+                second_level(q, minus8[q], turned[q])
+            q = step - 2 * LAG
+            if q >= 0:
+                raw_rate(q)
+
+        for h in range(2):
+            for t in range(PACK):
+                nc.scalar.activation(
+                    fetched[h][:, t * HALF : (t + 1) * HALF],
+                    gain[:, t * S : (t + 1) * S].indirect(itf_sb[:, h * cols : (h + 1) * cols]),
+                    ACT.Copy,
+                )
+        for q in range(NQ):
+            nc.scalar.activation(
+                out=part(fetched4, q, Q).rearrange("p (j t) -> p j t", t=PACK),
+                in_=fetched[q // 2][:].rearrange("p (t j) -> p j t", t=PACK)[:, q % 2 * W : (q % 2 + 1) * W, :],
+                func=ACT.Copy,
+            )
+
         for d in range(D):
             for h in range(2):
                 src = vdt(raw, h, BIG)[:, :, d, :]
@@ -259,15 +276,20 @@ def tile_picked_ywater_shr_p_kernel(
                         op0=ALU.max, op1=ALU.add,
                     )
         for h in range(2):
-            nc.scalar.activation(out=part(log_den, h, SMALL), in_=part(acc[D - 1], h, SMALL), func=ACT.Ln)
-        nc.scalar.activation(out=rden[:], in_=log_den[:], func=ACT.Exp, scale=-1.0)
+            nc.scalar.activation(
+                out=part(log_den, h, SMALL), in_=part(acc[D - 1], h, SMALL), func=ACT.Abs_reciprocal_sqrt
+            )
+            nc.scalar.activation(out=part(rden1, h, SMALL), in_=part(log_den, h, SMALL), func=ACT.Square)
+            nc.vector.tensor_tensor(
+                out=vt(rden, h, SMALL), in0=vt(rden1, h, SMALL),
+                in1=unit_sb[:].unsqueeze(1).broadcast_to([P, SMALL // PACK, PACK]), op=ALU.mult,
+            )
         for h in range(2):
             nc.vector.scalar_tensor_tensor(
                 out=part(num, h, BIG), in0=part(raw, h, BIG), scalar=0.0, in1=part(fetched4, h, BIG),
                 op0=ALU.max, op1=ALU.mult,
             )
 
-        out3 = out.rearrange("(m p) j -> p m j", p=P)
         for q in range(NQ):
             hid = sb([P, Q], BF16, "hid%d" % q)
             codes = sb([P, W], U32, "codes%d" % q)
@@ -277,10 +299,10 @@ def tile_picked_ywater_shr_p_kernel(
                 op=ALU.mult,
             )
             nc.vector.quantize_mx(out=codes[:].bitcast(FP8X4), scales=scales[:], in_=hid[:])
-            bank = psum.tile([P, N // P, W], F32, name="o%d" % q)
             for m in range(N // P):
+                cells = bank([P, W], "cells%d%d" % (q, m))
                 nc.tensor.matmul_mx(
-                    out=bank[:, m, :],
+                    out=cells[:],
                     lhsT=w2w[:, 2 * P * m : 2 * P * (m + 1)].bitcast(FP4X4),
                     lhsT_scale=w2s[:, P * m : P * (m + 1)],
                     rhs=codes[:].bitcast(FP8X4),
@@ -288,6 +310,9 @@ def tile_picked_ywater_shr_p_kernel(
                     start=True,
                     stop=True,
                 )
-            res = sb([P, N // P, W], F32, "res%d" % q)
-            nc.scalar.copy(out=res[:], in_=bank[:])
-            nc.sync.dma_start(out=out3[:, :, q * W : (q + 1) * W], in_=res[:])
+                res = sb([P, W], F32, "res%d%d" % (q, m))
+                if q == NQ - 1 and m == 1:
+                    nc.vector.tensor_copy(out=res[:], in_=cells[:])
+                else:
+                    nc.scalar.copy(out=res[:], in_=cells[:])
+                nc.sync.dma_start(out=out[m * P : (m + 1) * P, q * W : (q + 1) * W], in_=res[:])

import math
from contextlib import ExitStack

import concourse.mybir as mybir
from concourse.masks import make_identity

K, T, S, D, N, H = 512, 2048, 512, 4, 256, 512
FLOPS = 2 * K * H * S + 2 * H * N * S

F32 = mybir.dt.float32
BF16 = mybir.dt.bfloat16
I32 = mybir.dt.int32
U32 = mybir.dt.uint32
U16 = mybir.dt.uint16
U8 = mybir.dt.uint8
FP8X4 = mybir.dt.float8_e4m3fn_x4
FP4X4 = mybir.dt.float4_e2m1fn_x4
ACT = mybir.ActivationFunctionType
ALU = mybir.AluOpType

P = 128
PACK = 4
HALF = S // 2
LIST = 16
W = 128
NQ = S // W
Q = PACK * W
EXP_CAP = 2.0 ** 60
GAIN_FLOOR = 0.2


def tile_picked_ywater_shr_p_kernel(
    tc, x_words, x_scales, w1_words, w1_scales, noise, unit, w2_words, w2_scales, offs, itf, out
):
    nc = tc.nc
    with ExitStack() as ctx:
        keep = ctx.enter_context(tc.tile_pool(name="keep", bufs=1))
        psum = ctx.enter_context(tc.psum_pool(name="psum", bufs=1))

        def sb(shape, dtype, name):
            return keep.tile(shape, dtype, name=name, align_bytes=64)

        def load_scale_rows(queues, plane, rows):
            for q, queue in enumerate(queues):
                queue.dma_start(
                    out=plane[32 * q : 32 * q + 4, :].bitcast(I32), in_=rows[0, 4 * q : 4 * q + 4, :].bitcast(I32)
                )

        def shared(shape, dtype, name, tag):
            return keep.tile(shape, dtype, name=name, tag=tag, align_bytes=64)

        offs_sb = sb([P, S // LIST], U16, "offs_sb")
        itf_sb = sb([P, S // LIST], U16, "itf_sb")
        xw = sb([P, T], I32, "xw")
        xs = sb([P, T], U8, "xs")
        w1w_raw = sb([P, 2 * H], U8, "w1w_raw")
        w1s_raw = shared([P, H], U8, "w1s_raw", "early")
        unit_sb = sb([P, PACK], F32, "unit_sb")

        nc.vector.memset(xs[:, : T // 2].bitcast(I32), 0)
        nc.gpsimd.memset(xs[:, T // 2 :].bitcast(I32), 0)
        nc.gpsimd.memset(w1s_raw[:].bitcast(I32), 0)

        nc.sync.dma_start(offs_sb[:], offs)
        nc.sync.dma_start(out=w1w_raw[:].bitcast(I32), in_=w1_words[0].bitcast(I32))
        load_scale_rows([nc.sync] * 4, xs, x_scales)
        nc.sync.dma_start(out=xw[:], in_=x_words[0].rearrange("p n t -> p (n t)").bitcast(I32))
        load_scale_rows([nc.sync] * 4, w1s_raw, w1_scales)
        nc.sync.dma_start(itf_sb[:], itf)
        nc.sync.dma_start(out=unit_sb[:], in_=unit.rearrange("(p t) o -> p (t o)", t=PACK))

        w1w = sb([P, 2 * H], U8, "w1w")
        w1s = sb([P, H], U8, "w1s")
        nc.vector.tensor_copy(
            out=w1w[:].rearrange("p (t m b) -> p t m b", t=PACK, b=2),
            in_=w1w_raw[:].rearrange("p (m t b) -> p t m b", t=PACK, b=2),
        )
        nc.gpsimd.tensor_copy(
            out=w1s[:].rearrange("p (t m) -> p t m", t=PACK), in_=w1s_raw[:].rearrange("p (m t) -> p t m", t=PACK)
        )

        noise_sb = shared([P, PACK * S], F32, "noise_sb", "early")
        nc.sync.dma_start(out=noise_sb[:], in_=noise.rearrange("(p t) j -> p (t j)", t=PACK))

        def bank(shape, name):
            return psum.tile(shape, F32, name=name, tag="bank", bufs=8)

        ident = sb([P, P], F32, "ident")
        make_identity(nc, ident[:])

        cols = HALF // LIST
        e = shared([P, PACK * S], F32, "e", "exp")
        xg_s = [sb([P, HALF], U8, "xg_s%d" % h) for h in range(2)]
        xg_w = [sb([P, HALF], U32, "xg_w%d" % h) for h in range(2)]
        for h in range(2):
            nc.vector.tensor_copy(xg_s[h][:], xs[:].indirect(offs_sb[:, h * cols : (h + 1) * cols]))
        for h in range(2):
            nc.vector.tensor_copy(xg_w[h][:], xw[:].bitcast(U32).indirect(offs_sb[:, h * cols : (h + 1) * cols]))
        y = [bank([P, S], "y%d" % t) for t in range(PACK)]
        for t, h in [(0, 0), (1, 0), (0, 1), (1, 1), (2, 0), (2, 1), (3, 0), (3, 1)]:
            nc.tensor.matmul_mx(
                out=y[t][:, h * HALF : (h + 1) * HALF],
                lhsT=w1w[:, 2 * P * t : 2 * P * (t + 1)].bitcast(FP4X4),
                lhsT_scale=w1s[:, P * t : P * (t + 1)],
                rhs=xg_w[h][:].bitcast(FP8X4),
                rhs_scale=xg_s[h][:],
                start=True,
                stop=True,
            )
        for t in range(PACK):
            nc.scalar.activation(out=e[:, t * S : (t + 1) * S], in_=y[t][:], func=ACT.Exp)
        ec = shared([P, PACK * S], F32, "ec", "capped")
        for t in range(PACK):
            nc.vector.tensor_scalar(
                out=ec[:, t * S : (t + 1) * S], in0=e[:, t * S : (t + 1) * S], scalar1=EXP_CAP, scalar2=None, op0=ALU.min
            )

        soft = sb([P, PACK * S], F32, "soft")
        gain = sb([P, PACK * S], F32, "gain")
        c = math.exp(GAIN_FLOOR)
        for t in range(PACK):
            nc.scalar.activation(
                out=soft[:, t * S : (t + 1) * S], in_=ec[:, t * S : (t + 1) * S], func=ACT.Ln, scale=c, bias=c
            )
        for t in range(PACK):
            nc.vector.scalar_tensor_tensor(
                out=gain[:, t * S : (t + 1) * S], in0=y[t][:], scalar=GAIN_FLOOR, in1=soft[:, t * S : (t + 1) * S],
                op0=ALU.add, op1=ALU.max,
            )

        w2w = shared([P, 2 * N], U8, "w2w", "exp")
        w2s = shared([P, N], U8, "w2s", "capped")
        nc.gpsimd.memset(w2s[:].bitcast(I32), 0)
        nc.sync.dma_start(out=w2w[:].bitcast(I32), in_=w2_words[0].bitcast(I32))
        load_scale_rows([nc.sync] * 4, w2s, w2_scales)

        def part(tile, h, width):
            return tile[:, h * width : (h + 1) * width]

        def vdt(tile, q, width):
            return part(tile, q, width).rearrange("p (v d t) -> p v d t", d=D, t=PACK)

        def vt(tile, q, width):
            return part(tile, q, width).rearrange("p (v t) -> p v t", t=PACK)

        def over_d(tile, q, width):
            return vt(tile, q, width).unsqueeze(2).broadcast_to([P, width // PACK, D, PACK])

        def pairs_of(tile, q):
            return tile[:].rearrange("p (t q u e) -> p q t u e", t=PACK, q=NQ, e=2)[:, q]

        BIG = PACK * HALF
        SMALL = BIG // D
        V = W // D
        pair = sb([P, PACK * S // 2], F32, "pair")
        power = sb([P, S], F32, "power")
        cross = sb([P, PACK * S], F32, "cross")
        inv = sb([P, PACK * S], F32, "inv")
        low = sb([P, PACK * S], F32, "low")
        log_inv = sb([P, PACK * S], F32, "log_inv")
        raw = sb([P, PACK * S], F32, "raw")
        fetched = [sb([P, PACK * HALF], F32, "fetched%d" % h) for h in range(2)]
        fetched4 = sb([P, PACK * S], F32, "fetched4")
        acc = [sb([P, S], F32, "acc%d" % d) for d in range(D)]
        log_den = sb([P, S], F32, "log_den")
        rden = sb([P, S], F32, "rden")
        rden1 = sb([P, S], F32, "rden1")
        num = sb([P, PACK * S], F32, "num")

        def dg(tile, q):
            return part(tile, q, Q).rearrange("p (d g) -> p d g", d=D)

        def scaled_inverse(q):
            g = pairs_of(gain, q)
            nc.vector.tensor_tensor(
                out=part(pair, q, Q // 2).rearrange("p (t u) -> p t u", t=PACK), in0=g[:, :, :, 0], in1=g[:, :, :, 1],
                op=ALU.mult,
            )
            nc.vector.tensor_tensor(
                out=part(cross, q, Q).rearrange("p (e t u) -> p e t u", t=PACK, e=2),
                in0=pairs_of(noise_sb, q).rearrange("p t u e -> p e t u"),
                in1=g.rearrange("p t u e -> p e t u")[:, ::-1], op=ALU.mult,
            )
            halves = part(pair, q, Q // 2).rearrange("p (g h) -> p h g", h=2)
            nc.vector.scalar_tensor_tensor(
                out=part(power, q, W), in0=halves[:, 0, :], scalar=2.0, in1=halves[:, 1, :], op0=ALU.mult, op1=ALU.mult
            )
            nc.vector.tensor_tensor(
                out=part(inv, q, Q).rearrange("p (h e g) -> p h e g", h=2, e=2),
                in0=part(cross, q, Q).rearrange("p (e g h) -> p h e g", h=2, e=2),
                in1=halves[:, ::-1, :].unsqueeze(2).broadcast_to([P, 2, 2, W]),
                op=ALU.mult,
            )

        def add_turned(members, name):
            total = bank([P, W], name)
            for n, member in enumerate(members):
                nc.tensor.matmul(
                    total[:], lhsT=member, rhs=ident[:], is_transpose=True, start=(n == 0), stop=(n == len(members) - 1)
                )
            return total

        def first_level(q, minus8):
            total = add_turned([part(power, q, W)] + [dg(inv, q)[:, d, :] for d in range(D)], "first%d" % q)
            nc.scalar.activation(out=minus8, in_=total[:], func=ACT.Copy, scale=-2.0)
            turned = bank([P, D, W], "turned%d" % q)
            for d in range(D):
                nc.tensor.transpose(turned[:, d, :], dg(inv, q)[:, d, :], ident[:])
            return turned

        def second_level(q, minus8, turned):
            nc.vector.scalar_tensor_tensor(
                out=dg(low, q), in0=minus8.unsqueeze(1).broadcast_to([P, D, W]), scalar=-0.125, in1=turned[:],
                op0=ALU.mult, op1=ALU.max,
            )
            total = add_turned([minus8] + [dg(low, q)[:, d, :] for d in range(D)], "second%d" % q)
            nc.scalar.activation(
                out=vt(log_lvl[q], 0, W), in_=total[:].rearrange("p (t v) -> p v t", t=PACK), func=ACT.Ln, scale=-0.25
            )

        def log_of_inverse(q):
            nc.scalar.activation(
                out=part(log_inv, q, Q).rearrange("p (v d t) -> p d v t", d=D, t=PACK),
                in_=part(inv, q, Q).rearrange("p (d t v) -> p d v t", d=D, t=PACK),
                func=ACT.Ln,
            )

        def raw_rate(q):
            nc.vector.tensor_tensor(
                out=vdt(raw, q, Q), in0=over_d(log_lvl[q], 0, W), in1=vdt(log_inv, q, Q), op=ALU.subtract
            )

        spare = sb([P, 2 * W], F32, "spare")
        log_lvl = [
            fetched4[:, Q - W // 2 : Q + W // 2], fetched4[:, 3 * Q - W // 2 : 3 * Q + W // 2], spare[:, :W], spare[:, W:]
        ]
        minus8 = [fetched[1][:, q * HALF : q * HALF + W] for q in range(NQ)]
        turned = {}
        LAG = 2
        for step in range(NQ + 2 * LAG):
            if step < NQ:
                scaled_inverse(step)
                turned[step] = first_level(step, minus8[step])
                log_of_inverse(step)
            q = step - LAG
            if 0 <= q < NQ:
                second_level(q, minus8[q], turned[q])
            q = step - 2 * LAG
            if q >= 0:
                raw_rate(q)

        for h in range(2):
            for t in range(PACK):
                nc.scalar.activation(
                    fetched[h][:, t * HALF : (t + 1) * HALF],
                    gain[:, t * S : (t + 1) * S].indirect(itf_sb[:, h * cols : (h + 1) * cols]),
                    ACT.Copy,
                )
        for q in range(NQ):
            nc.scalar.activation(
                out=part(fetched4, q, Q).rearrange("p (j t) -> p j t", t=PACK),
                in_=fetched[q // 2][:].rearrange("p (t j) -> p j t", t=PACK)[:, q % 2 * W : (q % 2 + 1) * W, :],
                func=ACT.Copy,
            )

        for d in range(D):
            for h in range(2):
                src = vdt(raw, h, BIG)[:, :, d, :]
                if d == 0:
                    nc.vector.tensor_scalar(
                        out=vt(acc[d], h, SMALL), in0=src, scalar1=0.0, scalar2=0.5, op0=ALU.max, op1=ALU.add
                    )
                else:
                    nc.vector.scalar_tensor_tensor(
                        out=vt(acc[d], h, SMALL), in0=src, scalar=0.0, in1=vt(acc[d - 1], h, SMALL),
                        op0=ALU.max, op1=ALU.add,
                    )
        for h in range(2):
            nc.scalar.activation(
                out=part(log_den, h, SMALL), in_=part(acc[D - 1], h, SMALL), func=ACT.Abs_reciprocal_sqrt
            )
            nc.scalar.activation(out=part(rden1, h, SMALL), in_=part(log_den, h, SMALL), func=ACT.Square)
            nc.vector.tensor_tensor(
                out=vt(rden, h, SMALL), in0=vt(rden1, h, SMALL),
                in1=unit_sb[:].unsqueeze(1).broadcast_to([P, SMALL // PACK, PACK]), op=ALU.mult,
            )
        for h in range(2):
            nc.vector.scalar_tensor_tensor(
                out=part(num, h, BIG), in0=part(raw, h, BIG), scalar=0.0, in1=part(fetched4, h, BIG),
                op0=ALU.max, op1=ALU.mult,
            )

        for q in range(NQ):
            hid = sb([P, Q], BF16, "hid%d" % q)
            codes = sb([P, W], U32, "codes%d" % q)
            scales = sb([P, W], U8, "scales%d" % q)
            nc.vector.tensor_tensor(
                out=hid[:].rearrange("p (v d t) -> p v d t", d=D, t=PACK), in0=vdt(num, q, Q), in1=over_d(rden, q, W),
                op=ALU.mult,
            )
            nc.vector.quantize_mx(out=codes[:].bitcast(FP8X4), scales=scales[:], in_=hid[:])
            for m in range(N // P):
                cells = bank([P, W], "cells%d%d" % (q, m))
                nc.tensor.matmul_mx(
                    out=cells[:],
                    lhsT=w2w[:, 2 * P * m : 2 * P * (m + 1)].bitcast(FP4X4),
                    lhsT_scale=w2s[:, P * m : P * (m + 1)],
                    rhs=codes[:].bitcast(FP8X4),
                    rhs_scale=scales[:],
                    start=True,
                    stop=True,
                )
                res = sb([P, W], F32, "res%d%d" % (q, m))
                if q == NQ - 1 and m == 1:
                    nc.vector.tensor_copy(out=res[:], in_=cells[:])
                else:
                    nc.scalar.copy(out=res[:], in_=cells[:])
                nc.sync.dma_start(out=out[m * P : (m + 1) * P, q * W : (q + 1) * W], in_=res[:])
